import numpy as np
import ml_dtypes

BF16 = ml_dtypes.bfloat16


def bf(x):
    return np.asarray(x, np.float32).astype(BF16)


def f32(x):
    return np.asarray(x, np.float32)


def f64(x):
    return np.asarray(x).astype(np.float64)


def striped(idx):
    return np.concatenate([l.reshape(-1, 16).T for l in idx])


def rows(idx, k):
    return np.tile(np.repeat(idx, 16, axis=0), (k // (16 * 8), 1))


K, S, V, N = 128, 2048, 1024, 1024


def setup_inputs():
    return {"base": f32(np.random.standard_normal((K, S))), "v": f32(np.random.standard_normal((K, V))), "offs": striped(np.stack([np.random.permutation(S)[:N] for _ in range(8)]))}


def reference(base, v, offs):
    idx = np.stack([g.T.reshape(-1) for g in np.split(offs, 8)])
    x = f64(base).copy()
    np.put_along_axis(x, rows(idx, len(x)), np.tanh(f64(v)), axis=1)
    return x

@@ -1,0 +1,23 @@
+import concourse.mybir as mybir
+
+F32, U16 = mybir.dt.float32, mybir.dt.uint16
+TANH = mybir.ActivationFunctionType.Tanh
+GROUP = 16
+PIECE = 512
+
+
+def tile_lookup_put_tanh_out_kernel(tc, base, v, offs, out):
+    nc = tc.nc
+    rows, places = base.shape
+    entries = v.shape[1]
+    with tc.tile_pool(name="held", bufs=1) as held:
+        offsets = held.tile([rows, entries // GROUP], U16, name="offsets")
+        x = held.tile([rows, places], F32, name="x")
+        values = held.tile([rows, entries], F32, name="values")
+        nc.sync.dma_start(offsets[:], offs)
+        nc.sync.dma_start(x[:], base)
+        nc.sync.dma_start(values[:], v)
+        for first in range(0, entries, PIECE):
+            piece_offsets = offsets[:, first // GROUP : (first + PIECE) // GROUP]
+            nc.scalar.activation(x[:].indirect(piece_offsets), values[:, first : first + PIECE], TANH)
+        nc.sync.dma_start(out, x[:])

@@ -14,9 +14,17 @@ def tile_lookup_put_tanh_out_kernel(tc, base, v, offs, out):
         offsets = held.tile([rows, entries // GROUP], U16, name="offsets")
         x = held.tile([rows, places], F32, name="x")
         values = held.tile([rows, entries], F32, name="values")
-        nc.sync.dma_start(offsets[:], offs)
+        warm_in = held.tile([rows, 1], F32, name="warm_in")
+        warm_out = held.tile([rows, 1], F32, name="warm_out")
+
         nc.sync.dma_start(x[:], base)
-        nc.sync.dma_start(values[:], v)
+        nc.sync.dma_start(offsets[:], offs)
+        for first in range(0, entries, PIECE):
+            nc.sync.dma_start(values[:, first : first + PIECE], v[:, first : first + PIECE])
+
+        nc.vector.memset(warm_in[:], 0.0)
+        nc.scalar.activation(warm_out[:], warm_in[:], TANH)
+
         for first in range(0, entries, PIECE):
             piece_offsets = offsets[:, first // GROUP : (first + PIECE) // GROUP]
             nc.scalar.activation(x[:].indirect(piece_offsets), values[:, first : first + PIECE], TANH)

@@ -18,9 +18,9 @@ def tile_lookup_put_tanh_out_kernel(tc, base, v, offs, out):
         warm_out = held.tile([rows, 1], F32, name="warm_out")
 
         nc.sync.dma_start(x[:], base)
+        nc.scalar.dma_start(values[:, :PIECE], v[:, :PIECE])
         nc.sync.dma_start(offsets[:], offs)
-        for first in range(0, entries, PIECE):
-            nc.sync.dma_start(values[:, first : first + PIECE], v[:, first : first + PIECE])
+        nc.sync.dma_start(values[:, PIECE:], v[:, PIECE:])
 
         nc.vector.memset(warm_in[:], 0.0)
         nc.scalar.activation(warm_out[:], warm_in[:], TANH)
@@ -28,4 +28,7 @@ def tile_lookup_put_tanh_out_kernel(tc, base, v, offs, out):
         for first in range(0, entries, PIECE):
             piece_offsets = offsets[:, first // GROUP : (first + PIECE) // GROUP]
             nc.scalar.activation(x[:].indirect(piece_offsets), values[:, first : first + PIECE], TANH)
-        nc.sync.dma_start(out, x[:])
+
+        half = places // 2
+        nc.scalar.dma_start(out[:, :half], x[:, :half])
+        nc.sync.dma_start(out[:, half:], x[:, half:])

import concourse.mybir as mybir

F32, U16 = mybir.dt.float32, mybir.dt.uint16
TANH = mybir.ActivationFunctionType.Tanh
GROUP = 16
PIECE = 512


def tile_lookup_put_tanh_out_kernel(tc, base, v, offs, out):
    nc = tc.nc
    rows, places = base.shape
    entries = v.shape[1]
    with tc.tile_pool(name="held", bufs=1) as held:
        offsets = held.tile([rows, entries // GROUP], U16, name="offsets")
        x = held.tile([rows, places], F32, name="x")
        values = held.tile([rows, entries], F32, name="values")
        warm_in = held.tile([rows, 1], F32, name="warm_in")
        warm_out = held.tile([rows, 1], F32, name="warm_out")

        nc.sync.dma_start(x[:], base)
        nc.scalar.dma_start(values[:, :PIECE], v[:, :PIECE])
        nc.sync.dma_start(offsets[:], offs)
        nc.sync.dma_start(values[:, PIECE:], v[:, PIECE:])

        nc.vector.memset(warm_in[:], 0.0)
        nc.scalar.activation(warm_out[:], warm_in[:], TANH)

        for first in range(0, entries, PIECE):
            piece_offsets = offsets[:, first // GROUP : (first + PIECE) // GROUP]
            nc.scalar.activation(x[:].indirect(piece_offsets), values[:, first : first + PIECE], TANH)

        half = places // 2
        nc.scalar.dma_start(out[:, :half], x[:, :half])
        nc.sync.dma_start(out[:, half:], x[:, half:])
